import numpy as np, ml_dtypes
CORES = [16,18,20,22]
N = 4
BF = ml_dtypes.bfloat16
W, L, S, T, F = 4096, 256, 1, 5, 256
C = W >> S
LEVELS = np.array([800, 900, 1000, 1050, 1100, 1150, 1250, 1400])
def parts(rng):
    d = {"key": rng.integers(0, 256, (N, 8, 16, W)), "em": rng.integers(0, 256, (N, 8, 16, W)), "cl": rng.integers(0, W, (N, 8, 16, C)), "pl": rng.integers(0, W, (N, 8, 16, L)),
         "q": rng.integers(0, 256, (N, 8, 16, L)), "emb": rng.integers(0, 256, (N, 8, 16, 16)), "w": rng.integers(0, 256, (N, 8, 16, 1))}
    base = np.stack([rng.permutation(LEVELS) for r in range(N)]).reshape(N, 8, 1, 1)
    d["th"] = base + rng.integers(-100, 101, (N, 8, 16, 1))
    return d
def pack(d):
    kinds = {"key": BF, "em": BF, "cl": np.int32, "pl": np.int32, "q": BF, "emb": BF, "w": BF, "th": np.float32}
    return {k: np.ascontiguousarray(d[k].reshape(N, 128, -1)).astype(np.float32).astype(t) for k, t in kinds.items()}
def setup_inputs(rng):
    return pack(parts(rng))
def setup_inputs_ties(rng):
    d = parts(rng); o = rng.permutation(8)
    for k in ("key", "q", "emb"): d[k] = 64 * rng.integers(0, 4, d[k].shape)
    d["th"] = 64 * rng.integers(16, 23, (N, 8, 16, 1)) + rng.integers(0, 2, (N, 8, 16, 1))
    d["em"] = rng.integers(0, 2, (N, 8, 16, W)) * rng.choice(np.array([1, 3, 255]), (N, 8, 1, 1))
    d["em"][:, o[0]] = 7; d["em"][:, o[1]] = 0
    for k in ("key", "q", "emb"):
        d[k][:, o[2]] = 0
        d[k][:, o[3]] = rng.integers(0, 32, d[k][:, o[3]].shape)
    d["th"][:, o[2], :, 0] = rng.permutation(np.arange(16) % 3)
    d["th"][:, o[3]] = rng.integers(1, 256, (N, 16, 1))
    return pack(d)
def setup_inputs_ends(rng):
    d = parts(rng); o = rng.permutation(8); ends = np.array([0, 1, W - 2, W - 1])
    d["pl"][:, o[0]] = rng.choice(ends, (N, 16, L)); d["th"][:, o[0]] = 4096
    d["th"][:, o[1]] = 0
    d["pl"][:, o[2]] = rng.integers(0, W, (N, 1, L))
    d["cl"][:, o[3]] = rng.choice(ends, (N, 16, C)); d["th"][:, o[3]] = 1000
    d["cl"][:, o[4]] = rng.integers(0, W, (N, 1, C))
    d["key"][:, o[5]] = d["key"][:, o[5]][:, :, :1]
    d["pl"][:, o[6]] = rng.choice(ends, (N, 16, L))
    d["th"][:, o[7]] = 0; d["w"][:, o[7]] = 0
    return pack(d)
def setup_inputs_lone(rng):
    d = parts(rng); d["th"] = np.zeros((N, 8, 16, 1), np.int64)
    for r in range(N):
        o = rng.permutation(8)
        d["th"][r, o[1], 0] = 4096; d["th"][r, o[2], 15] = 4096; d["th"][r, o[3], 14:] = 4096
        for g in o[4:]: d["th"][r, g, rng.integers(1, 15)] = 4096
    d["th"][rng.integers(0, N)] = 0
    return pack(d)
def setup_inputs_big(rng):
    d = parts(rng); o = rng.permutation(8)
    for k in ("key", "em", "q", "emb"): d[k] = 255 * rng.integers(0, 2, d[k].shape)
    d["w"] = rng.integers(254, 256, d["w"].shape)
    d["th"] = rng.choice(np.array([1785, 1786, 2040, 2041, 2295, 1020, 4080, 4081]), (N, 8, 16, 1))
    d["key"][:, o[0]] = 0; d["q"][:, o[0]] = 255; d["emb"][:, o[0]] = 255; d["w"][:, o[0]] = 255
    d["th"][:, o[0], :, 0] = 4080 + np.arange(16) % 2
    d["em"][:, o[1]] = 255
    d["th"][:, o[2]] = 0
    d["th"][:, o[3]] = 0; d["q"][:, o[3]] = 255; d["emb"][:, o[3]] = 255; d["w"][:, o[3]] = 255
    d["em"][:, o[4]] = 255 - (rng.random((N, 16, W)) < 0.0625)
    return pack(d)
def setup_inputs_spread(rng):
    d = parts(rng)
    for k in ("key", "em", "q", "emb"):
        s = d[k].shape
        d[k] = np.minimum((np.exp2(10 * rng.random(s[:2] + (1, s[3]))) * rng.random(s)).astype(np.int64), 255)
    d["w"] = np.minimum(np.exp2(8 * rng.random(d["w"].shape)).astype(np.int64), 255)
    d["th"] = np.minimum(np.exp2(8 + 4 * rng.random((N, 8, 16, 1))).astype(np.int64), 4096)
    for k in ("pl", "cl"): d[k] = np.minimum((W * rng.random(d[k].shape) ** 3).astype(np.int64), W - 1)
    return pack(d)
def check_inputs(d):
    bad = []
    for k, hi in (("key", 255), ("em", 255), ("cl", W - 1), ("pl", W - 1), ("q", 255), ("emb", 255), ("w", 255), ("th", 4096)):
        a = np.asarray(d[k]).astype(np.float64)
        if not np.all((a >= 0) & (a <= hi) & (a == np.floor(a))): bad.append("whole numbers and range of " + k)
    return bad
def reference(key, em, cl, pl, q, emb, w, th):
    def ints(a): return a.astype(np.float32).astype(np.int32).reshape(N, 8, 16, -1)
    K, E, CL, B, H, TH = ints(key), ints(em), ints(cl), ints(emb), ints(w), ints(th)
    p, x = ints(pl), ints(q)
    toks = [[] for r in range(N)]
    for t in range(T):
        pn, xn = [], []
        for r in range(N):
            at = np.take_along_axis(K[r], p[r].reshape(8, 1, 16 * L), 2).reshape(8, 16, 16, L)
            dist = np.add.reduce(np.abs(at - x[r][:, :, None, :]), axis=1)
            near = dist < TH[r]
            first = np.argmax(near, axis=1)
            lead = np.take_along_axis(p[r], first[:, None, :], 1)[:, 0]
            h = np.add.reduce(H[r] * x[r], axis=1)
            c = np.where(np.any(near, axis=1), lead >> S, h & (C - 1))
            pr = np.where(near, p[r], np.take_along_axis(CL[r], c[:, None, :], 2))
            v = np.add.reduce(np.take_along_axis(E[r], pr.reshape(8, 1, 16 * L), 2).reshape(8, 16, 16, L), axis=2)
            tok = np.argmax(v, axis=1)
            toks[r].append(tok)
            xn.append((x[r] + np.take_along_axis(B[r], tok[:, :, None], 1).transpose(0, 2, 1)) >> 1); pn.append(pr)
        p = np.stack([np.concatenate([(pn[(r - 1) % N][..., :F] + (1 if r == 0 else 0)) & (W - 1), (pn[(r + 1) % N][..., F:] - (1 if r == N - 1 else 0)) & (W - 1)], axis=2) for r in range(N)])
        x = np.stack([np.concatenate([xn[(r - 1) % N][..., :F], xn[(r + 1) % N][..., F:]], axis=2) for r in range(N)])
    yt = np.stack([np.concatenate(a, axis=1) for a in toks])
    return {"yp": p.reshape(N, 128, L).astype(np.float32), "yq": x.reshape(N, 128, L).astype(np.float32).astype(BF), "yt": yt.astype(np.float32)}

from concourse.bass import DstId, RemoteDMATransfer
from concourse.mybir import AluOpType, ActivationFunctionType

STEPS, CH, NL = 5, 2, 128
NP = 4
KB = 4096.0
MAGIC = 8388608.0
HUGE = 25769803776.0
CYC, PEC, GAT, HOP, NET = 1.0, 0.5, 1.6, 60.0, 2200.0
ITERS, TEMP = 40000, 600.0

SCRATCH = {"e8": ("sbuf", [8, 128], "bfloat16"), "ytb": ("sbuf", [8, 1280], "float32")}


def _declare(where, dtype, names, cols, per_chunk=False):
    for nm in names.split():
        for x in (range(CH) if per_chunk else [""]):
            SCRATCH["%s%s" % (nm, x)] = (where, [128, cols], dtype)


_declare("sbuf", "bfloat16", "keyt emt", 4112)
_declare("sbuf", "int32", "clt", 2056)
_declare("sbuf", "int32", "plt fi fj", 256)
_declare("sbuf", "float32", "ff", 256)
_declare("sbuf", "float32", "tht kcf cc wf", 1)
_declare("sbuf", "int32", "kci kcj", 1)
_declare("sbuf", "bfloat16", "wt", 1)
_declare("sbuf", "bfloat16", "embt", 16)
_declare("sbuf", "float16", "embs", 16)
_declare("sbuf", "bfloat16", "lq", 1536)
_declare("sbuf", "float16", "lp", 1536)
_declare("sbuf", "uint16", "lu", 1536)
_declare("sbuf", "bfloat16", "sq", 1280)
_declare("sbuf", "float16", "sp sp1", 1280)
_declare("sbuf", "uint16", "su su1", 1280)
_declare("sbuf", "bfloat16", "ones idm bma bm ltm lw nid hid mid sid kid bk bgi bg", 128)
_declare("sbuf", "bfloat16", "gw gk kv", 8)
_declare("sbuf", "int32", "mki mkj", 128)
_declare("sbuf", "float32", "mk z0 z1", 128)
_declare("sbuf", "float16", "ebk", 128)
_declare("sbuf", "bfloat16", "sl", 2048)
_declare("psum", "float32", "x0 x1 x2 x3", 512)
_declare("psum", "float32", "A B", 512, True)
_declare("sbuf", "bfloat16", "kg", 4096, True)
_declare("sbuf", "bfloat16", "ab eg", 2048, True)
_declare("sbuf", "float32", "hi", 8, True)
_declare("sbuf", "float16", "hf", 8, True)
_declare("sbuf", "uint16", "ls", 8, True)
_declare("sbuf", "bfloat16", "far oh on", 128, True)
_declare("sbuf", "float16", "sel prd vm", 128, True)
_declare("sbuf", "float32", "g1 bs", 128, True)
_declare("sbuf", "float32", "fm", 144, True)
for _c in range(CH):
    SCRATCH["def%d" % _c] = ("sbuf", [8, 128], "float16")

SEMAPHORES = ["V", "S", "P", "G", "lsem", "ld_pl", "ld_q", "ld_key", "ld_sm", "ld_cl", "ld_em", "st"]
for _t in range(STEPS):
    for _c in range(CH):
        SEMAPHORES += ["ap%d%d" % (_t, _c), "aq%d%d" % (_t, _c)]


def make_ops(g, T, topo, core, rank):
    A, F = AluOpType, ActivationFunctionType
    V, S, P = g.vector, g.scalar, g.tensor
    ops = []

    def op(name, qs, fn, rd, wr, banks=(), cost=100.0, sem=None, lat=0.0, skip=False):
        ops.append(dict(name=name, qs=qs, fn=fn, rd=list(rd), wr=list(wr), banks=list(banks), cost=cost, sem=sem,
                        lat=lat, skip=skip, i=len(ops)))

    def vop(name, fn, rd, wr, n, banks=()):
        op(name, "V", lambda q: [fn()], rd, wr, banks, 55 + max(64, n) * CYC)

    def sop(name, fn, rd, wr, n, banks=()):
        op(name, "S", lambda q: [fn()], rd, wr, banks, 80 + n * CYC)

    def mm(name, mms, rd, wr, banks):
        op(name, "P", lambda q: [P.matmul(*m[:5]) for m in mms], rd, wr, banks, 10 + sum(max(64, m[5]) for m in mms) * PEC)

    def gop(name, fn, rd, wr, n):
        op(name, "G", lambda q: [fn()], rd, wr, (), 170 + 2 * n * CYC)

    def ld(name, q, pairs, wr, sem, lat, rd=()):
        eng = g.sync if q == "Y" else g.scalar
        op(name, q, lambda _q: [eng.dma_start(o, i) for o, i in pairs], rd, wr, (), 60.0 * len(pairs), sem, lat)

    ld("ld_pl", "Y", [(T.plt[:], T.pl[:])], ["plt"], "ld_pl", 2000)
    ld("ld_key", "Y", [(T.keyt[:, 0:4096], T.key[:]), (T.keyt[:, 4096:4098], T.key[:, 0:2])], ["keyt"], "ld_key", 4800)
    ld("ld_sm", "S", [(T.tht[:], T.th[:]), (T.wt[:], T.w[:]), (T.embt[:], T.emb[:])], ["tht", "wt", "embt"], "ld_sm", 2000)
    ld("ld_q", "S", [(T.lq[:, 0:256], T.q[:])], ["lq00", "lq01"], "ld_q", 2000)
    ld("ld_cl", "Y", [(T.clt[:, 0:2048], T.cl[:]), (T.clt[:, 2048:2050], T.cl[:, 0:2])], ["clt"], "ld_cl", 7500)
    ld("ld_em", "Y", [(T.emt[:, 0:4096], T.em[:]), (T.emt[:, 4096:4098], T.em[:, 0:2])], ["emt"], "ld_em", 10500)

    vop("ones", lambda: V.memset(T.ones[:], 1.0), [], ["ones"], 64)
    vop("slz", lambda: V.memset(T.sl[:], 0.0), [], ["sl"], 1024)
    for c in range(CH):
        a, b = c * NL, c * NL + NL
        vop("u0_%d" % c, lambda a=a, b=b: V.tensor_copy(T.lu[:, a:b], T.plt[:, a:b]), ["plt"], ["lu0%d" % c], 128)
        vop("p0_%d" % c, lambda a=a, b=b: V.tensor_scalar(T.lp[:, a:b], T.plt[:, a:b], -2048.0, None, A.add), ["plt"],
            ["lp0%d" % c], 128)

    def sel(name, src, pattern, cmp, base, cm, rows=128):
        gop(name, lambda: g.affine_select(T[name][:], T[src][0:rows, :], pattern, cmp, 0.0, base, cm), [src], [name], 128)

    def iota(name, pattern, base, cm, n=128, flag=True):
        kw = dict(allow_small_or_imprecise_dtypes=True) if flag else {}
        gop(name, lambda: g.iota(T[name][:], pattern, base, cm, **kw), [], [name], n)
    sel("idm", "ones", [[-1, 128]], A.is_equal, 0, 1)
    sel("bma", "ones", [[-16, 8], [0, 16]], A.is_ge, 0, 1)
    sel("bm", "bma", [[16, 8], [0, 16]], A.is_ge, 15, -1)
    sel("ltm", "bm", [[1, 128]], A.is_gt, 0, -1)
    iota("kci", [[0, 1]], 0, 1, 1, False)
    iota("mki", [[0, 8], [-1, 16]], 16, 1, 128, False)
    sel("e8", "ones", [[-1, 8], [0, 16]], A.is_equal, 0, 1, 8)
    iota("bk", [[0, 8], [-1, 16]], 15, 0)
    iota("bgi", [[1, 8], [0, 16]], 0, 0)

    def scaled(name, src, k):
        vop(name, lambda: V.tensor_scalar(T[name][:], T[src][:], float(k), None, A.mult), [src], [name], 64)
    scaled("nid", "idm", -1.0)
    for j in range(8):
        vop("sl%d" % j, lambda j=j: V.tensor_copy(T.sl[:, 16 * j:16 * j + 129 * 15 + 1:129], T.bm[:, 16 * j:16 * j + 16]),
            ["bm", "sl"], ["sl_%d" % j], 16)
    SLK = ["sl"] + ["sl_%d" % x for x in range(8)]
    scaled("hid", "idm", 0.5)
    scaled("mid", "idm", -2048.0)
    scaled("sid", "idm", 16.0)
    scaled("kid", "idm", KB)
    scaled("lw", "ltm", KB)
    vop("lw1", lambda: V.tensor_tensor(T.lw[:], T.lw[:], T.kid[:], A.subtract), ["lw", "kid"], ["lw"], 256)
    vop("wf", lambda: V.tensor_copy(T.wf[:], T.wt[:]), ["wt"], ["wf"], 1)
    vop("gw", lambda: V.tensor_scalar(T.gw[:], T.bm[:, 0::16], T.wf[:], None, A.mult), ["bm", "wf"], ["gw"], 8)
    vop("gk", lambda: V.tensor_scalar(T.gk[:], T.bm[:, 0::16], KB, None, A.mult), ["bm"], ["gk"], 8)
    vop("kcj", lambda: V.tensor_scalar(T.kcj[:], T.kci[:], 15, None, A.bitwise_and), ["kci"], ["kcj"], 1)
    vop("kcf", lambda: V.tensor_copy(T.kcf[:], T.kcj[:]), ["kcj"], ["kcf"], 1)
    vop("cc", lambda: V.tensor_scalar(T.cc[:], T.kcf[:], -KB, 1023.75, A.mult, A.add), ["kcf"], ["cc"], 1)
    vop("kv", lambda: V.tensor_scalar(T.kv[:], T.bm[:, 0::16], T.kcf[:], None, A.mult), ["bm", "kcf"], ["kv"], 8)
    vop("mkj", lambda: V.tensor_scalar(T.mkj[:], T.mki[:], 15, None, A.bitwise_and), ["mki"], ["mkj"], 128)
    vop("mk", lambda: V.tensor_scalar(T.mk[:], T.mkj[:], 0.0, None, A.is_equal), ["mkj"], ["mk"], 128)
    scaled("bg", "bgi", 65536.0)
    vop("embs", lambda: V.tensor_scalar(T.embs[:], T.embt[:], 0.5, -0.25, A.mult, A.add), ["embt"], ["embs"], 16)
    for j in range(8):
        vop("ebk%d" % j, lambda j=j: V.tensor_tensor(T.ebk[:, 16 * j:16 * j + 16], T.embs[:], T.bm[:, 16 * j:16 * j + 16],
                                                     A.mult), ["bm", "embs"], ["ebk_%d" % j], 32)
    EBK = ["ebk_%d" % x for x in range(8)]
    vop("z0", lambda: V.memset(T.z0[:], 0.0), [], ["z0"], 128)
    vop("z1", lambda: V.memset(T.z1[:], 0.0), [], ["z1"], 128)
    vop("z1b", lambda: V.memset(T.z1[:, 0::16], 4194304.0), ["z1"], ["z1"], 8)
    for c in range(CH):
        vop("fmt%d" % c, lambda c=c: V.memset(T["fm%d" % c][:, 128:144], 8388608.0), [], ["fmt%d" % c], 16)

    nxt = T.cores[(rank + 1) % len(T.cores)]
    rid, pid = topo.addr(nxt)[0], topo.addr(nxt)[1]
    eng = topo.engines(core, nxt)
    m_all, m_a, m_b = sum(1 << e for e in eng), sum(1 << e for e in eng[0::2]), sum(1 << e for e in eng[1::2])
    last_rank = rank == len(T.cores) - 1
    win_k, win_e, win_c = T.keyt[:, 0:4098], T.emt[:, 0:4098], T.clt[:, 0:2050]
    LP = NL // NP
    X = [T.x0, T.x1, T.x2, T.x3]

    def gather(name, dst, win, lst, rd, wr, n):
        def emit(q):
            if q == "V":
                return [V.tensor_copy(dst, win.indirect(lst))]
            return [S.activation(dst, win.indirect(lst), F.Copy)]
        op(name, "VS", emit, rd, wr, (), 60 + n * GAT)

    def step(t, c):
        n, nn = "%d%d" % (t, c), "%d%d" % (t + 1, c)
        o = t * 256 + c * NL
        here, dst = slice(o, o + NL), slice(o + 256, o + 256 + NL)
        p, q = T.lp[:, here], T.lq[:, here]
        Ab, Bb = T["A%d" % c], T["B%d" % c]
        bA, bB = "bA%d" % c, "bB%d" % c
        A1, A2, B0, B1 = "A1%d" % c, "A2%d" % c, "B0%d" % c, "B1%d" % c
        kg, ab, hi, hf, far, se, prd, vm, ls, g1, eg, fm, bs, oh, on, dfl = (T[x + str(c)] for x in (
            "kg ab hi hf far sel prd vm ls g1 eg fm bs oh on def".split()))

        def k(x):
            return "%s%d" % (x, c)
        ko = (t % 2) * 2048
        kr = ["kg%d%d_%d" % (c, t % 2, j) for j in range(NP)]
        for j in range(NP):
            gather("kg%s_%d" % (n, j), kg[:, ko + 16 * LP * j:ko + 16 * LP * (j + 1)], win_k,
                   T.lu[:, o + LP * j:o + LP * (j + 1)], ["keyt", "lu" + n], [kr[j]], 16 * LP)
        mm("h" + n, [(Bb[:, 128:136], q, T.gw[:], True, True, 8)], ["lq" + n, "gw"], [B1], [bB])
        vop("hi" + n, lambda: V.tensor_scalar(hi[:], Bb[:, 128:136], -1023.5, HUGE, A.add, A.add), [B1], [k("hi")], 8, [bB])
        vop("hf" + n, lambda: V.tensor_scalar(hf[:], hi[:], -HUGE, 1.0 / 2048.0, A.add, A.mult), [k("hi")], [k("hf")], 8)
        for b in range(4):
            mm("xk%s_%d" % (n, b), [(X[b][:, 128 * j:128 * j + 128], T.idm[:], kg[:, ko + 4 * b + j:ko + 2048:16], j == 0,
                                     False, 128) for j in range(4)], kr + ["idm"], ["x%d" % b], ["bx%d" % b])
        for b in range(4):
            mm("xq%s_%d" % (n, b), [(X[b][:, 128 * j:128 * j + 128], T.nid[:], q, False, j == 3, 128) for j in range(4)],
               ["lq" + n, "nid"], ["x%d" % b], ["bx%d" % b])
            sop("ab%s_%d" % (n, b), lambda b=b: S.activation(ab[:, 512 * b:512 * b + 512], X[b][:], F.Abs), ["x%d" % b],
                ["ab%d_%d" % (c, b)], 512, ["bx%d" % b])
            mm("d%s_%d" % (n, b), [(Ab[:, 0:128], T.sl[:, 128 * s:128 * s + 128], ab[:, 128 * s:128 * s + 128], s == 0,
                                    s == 15, 128) for s in range(4 * b, 4 * b + 4)], ["ab%d_%d" % (c, b)] + SLK, [k("d")], [bA])
        vop("far" + n, lambda: V.tensor_scalar(far[:], Ab[:, 0:128], T.tht[:], None, A.is_ge), [k("d"), "tht"], [k("far")],
            128, [bA])
        mm("y" + n, [(Bb[:, 0:128], T.hid[:], p, True, False, 128), (Bb[:, 0:128], T.lw[:], far[:], False, True, 128)],
           [k("far"), "lp" + n, "hid", "lw"], [B0], [bB])
        y2 = Ab[0:8, 384:512]
        mm("y2" + n, [(y2, T.gw[:], q, True, False, 128), (y2, hf[:], T.mid[:], False, False, 128),
                      (y2, T.gk[:], far[:], False, True, 128)],
           [k("far"), k("hf"), "lq" + n, "gw", "mid", "gk"], [k("y2")], [bA])
        mm("f2" + n, [(Ab[:, 128:256], T.idm[:], far[:], True, True, 128)], [k("far"), "idm"], [A1], [bA])
        vop("sel" + n, lambda: V.tensor_scalar(se[:], Bb[:, 0:128], T.cc[:], 0.0, A.add, A.max), [B0, "cc"], [k("sel")],
            128, [bB])
        vop("def" + n, lambda: V.tensor_scalar(dfl[:], y2, -16 * KB, 0.0, A.add, A.max), [k("y2")], [k("def")], 128, [bA])
        mm("ex" + n, [(Bb[:, 128:256], se[:], T.bm[:], True, False, 128), (Bb[:, 128:256], dfl[:], T.e8[:], False, True, 128)],
           [k("sel"), k("def"), "bm", "e8"], [B1], [bB])
        vop("prd" + n, lambda: V.tensor_tensor(prd[:], Ab[:, 128:256], p, A.mult), [A1, "lp" + n], [k("prd")], 128, [bA])
        vop("vm" + n, lambda: V.tensor_tensor(vm[:], Bb[:, 128:256], T.mk[:], A.mult), [B1, "mk"], [k("vm")], 128, [bB])
        mm("l" + n, [(Bb[:, 0:8], vm[:], T.bm[:, 0::16], True, True, 8)], [k("vm"), "bm"], [B0], [bB])
        z = Ab[:, 256:384]
        mm("z" + n, [(z, T.idm[:], p, True, False, 128), (z, T.mid[:], far[:], False, False, 128),
                     (z, T.nid[:], prd[:], False, True, 128)],
           ["lp" + n, k("far"), k("prd"), "idm", "mid", "nid"], [A2], [bA])
        vop("ls" + n, lambda: V.tensor_scalar(ls[:], Bb[:, 0:8], MAGIC, -MAGIC, A.add, A.add), [B0], [k("ls")], 8, [bB])
        vop("g1" + n, lambda: V.tensor_tensor(g1[:], win_c.indirect(ls[:]), far[:], A.mult), ["clt", k("ls"), k("far")],
            [k("g1")], 200)
        sp, su, sp1, su1 = T.sp[:, here], T.su[:, here], T.sp1[:, here], T.su1[:, here]
        vop("pn" + n, lambda: V.tensor_tensor(sp, g1[:], z, A.add), [k("g1"), A2], ["sp" + n], 128, [bA])
        vop("un" + n, lambda: V.tensor_scalar(su, sp, 2048.0, None, A.add), ["sp" + n], ["su" + n], 64)
        last = t == STEPS - 1
        op("up" + n, "V", lambda _q: [V.tensor_scalar(su1, sp, 2049.0, None, A.add)], ["sp" + n], ["su1" + n], (), 115,
           skip=not last_rank)
        if not last:
            op("pp" + n, "V", lambda _q: [V.tensor_scalar(sp1, sp, 1.0, None, A.add)], ["sp" + n], ["sp1" + n], (), 115,
               skip=not last_rank)
        hu, hp = (su1, sp1) if last_rank else (su, sp)

        def send_p(_q):
            if last:
                g.remote_dma(T.lu[:, dst], hu, T.sem["ap" + n], T.sem.lsem, pid, rid, m_all)
                return None
            g.remote_dma_fused([RemoteDMATransfer(dst_ids=[DstId(rid=rid, pnc=pid)], dma_engine_mask=m,
                                                  remote_sem=T.sem["ap" + n], src=s, dst=d)
                                for m, s, d in ((m_a, hu, T.lu[:, dst]), (m_b, hp, T.lp[:, dst]))], local_sem=T.sem.lsem)
            return None
        op("sendp" + n, "G", send_p, ["su" + n, "su1" + n] + ([] if last else ["sp" + n, "sp1" + n]),
           ["lu" + nn] + ([] if last else ["lp" + nn]), (), 150, "ap" + n, NET)
        if last:
            r = slice(c * NL, c * NL + NL)
            vop("fi%d" % c, lambda: V.tensor_copy(T.fi[:, r], T.lu[:, dst]), ["lu" + nn], [k("fi")], 128)
            vop("fj%d" % c, lambda: V.tensor_scalar(T.fj[:, r], T.fi[:, r], 4095, None, A.bitwise_and), [k("fi")], [k("fj")], 128)
            vop("ff%d" % c, lambda: V.tensor_copy(T.ff[:, r], T.fj[:, r]), [k("fj")], [k("ff")], 128)
            ld("stp%d" % c, "Y", [(T.yp[:, r], T.ff[:, r])], ["yp%d" % c], "st", 2000, [k("ff")])
        for j in range(NP):
            gather("eg%s_%d" % (n, j), eg[:, 16 * LP * j:16 * LP * (j + 1)], win_e, T.su[:, o + LP * j:o + LP * (j + 1)],
                   ["emt", "su" + n], ["eg%d_%d" % (c, j)], 16 * LP)
        v = Ab[:, 128:256]
        mm("v" + n, [(v, T.ones[0:1, :], T.bk[0:1, :], True, False, 128), (v, T.ones[0:1, :], T.bg[0:1, :], False, False, 128)]
           + [(v, eg[:, s::16], T.sid[:], False, s == 15, 128) for s in range(16)],
           ["eg%d_%d" % (c, j) for j in range(NP)] + ["ones", "bk", "bg", "sid"], [A1], [bA])
        vop("fm" + n, lambda: V.tensor_tensor_scan(fm[:, 0:128], T.z0[:], v, 0.0, A.add, A.max), [A1, "z0"], [k("fm")], 128, [bA])
        vop("bs" + n, lambda: V.tensor_tensor_scan(bs[:], T.z1[:], fm[:, 15:143], 0.0, A.add, A.min),
            [k("fm"), k("fmt"), "z1"], [k("bs")], 128)
        vop("oh" + n, lambda: V.tensor_tensor(oh[:], v, bs[:], A.is_equal), [A1, k("bs")], [k("oh")], 128, [bA])
        mm("on" + n, [(Bb[:, 256:384], oh[:], T.idm[:], True, True, 128)], [k("oh"), "idm"], [k("onp")], [bB])
        sop("ons" + n, lambda: S.activation(on[:], Bb[:, 256:384], F.Copy), [k("onp")], [k("on")], 128, [bB])
        e = Bb[:, 384:512]
        mm("e" + n, [(e, T.hid[:], q, True, False, 128), (e, T.ebk[:], on[:], False, True, 128)],
           ["lq" + n, k("on"), "hid"] + EBK, [k("e")], [bB])
        sq = T.sq[:, here]
        vop("qn" + n, lambda: V.tensor_scalar(sq, e, MAGIC, -MAGIC, A.add, A.add), [k("e")], ["sq" + n], 128, [bB])

        def send_q(_q):
            g.remote_dma(T.lq[:, dst], sq, T.sem["aq" + n], T.sem.lsem, pid, rid, m_all)
            return None
        op("sendq" + n, "G", send_q, ["sq" + n], ["lq" + nn], (), 150, "aq" + n, NET)
        mm("tk" + n, [(Ab[0:8, 256:384], T.kv[:], on[:], True, True, 128)], [k("on"), "kv"], [A2], [bA])
        sop("yt" + n, lambda: S.activation(T.ytb[:, here], Ab[0:8, 256:384], F.Copy), [A2], ["yt" + n], 128, [bA])
        if last:
            ld("stq%d" % c, "Y", [(T.yq[:, c * NL:c * NL + NL], T.lq[:, dst])], ["yq%d" % c], "st", 2000, ["lq" + nn])
            if c == CH - 1:
                ld("stt", "Y", [(T.yt[:], T.ytb[:])], ["ytd"], "st", 2000,
                   ["yt%d%d" % (x, y) for x in range(STEPS) for y in range(CH)])

    for t in range(STEPS):
        for c in range(CH):
            step(t, c)
    return ops


def depend(ops):
    wr, rds, bank = {}, {}, {}
    for o in ops:
        d = set()
        for k in o["rd"]:
            if k in wr:
                d.add(wr[k])
        for k in o["wr"]:
            if k in wr:
                d.add(wr[k])
            d.update(rds.get(k, ()))
        for b in o["banks"]:
            turn = bank.setdefault(b, ["", [], []])
            if turn[0] != o["qs"]:
                turn[0], turn[1], turn[2] = o["qs"], turn[2], []
            d.update(turn[1])
            turn[2].append(o["i"])
        for k in o["rd"]:
            rds.setdefault(k, []).append(o["i"])
        for k in o["wr"]:
            wr[k] = o["i"]
            rds[k] = []
        d.discard(o["i"])
        o["deps"] = sorted(d)


def schedule(ops):
    n = len(ops)
    succ = [[] for _ in ops]
    for o in ops:
        for d in o["deps"]:
            succ[d].append(o["i"])
    bl = [0.0] * n
    for i in range(n - 1, -1, -1):
        bl[i] = ops[i]["cost"] + ops[i]["lat"] + max([bl[s] + HOP for s in succ[i]] or [0.0])
    left = [len(o["deps"]) for o in ops]
    done, ready, free, order = [0.0] * n, {i: 0.0 for i in range(n) if left[i] == 0}, {}, []
    while ready:
        st, _, i, q = min((max(r, free.get(q, 0.0)), -bl[i], i, q) for i, r in ready.items() for q in ops[i]["qs"])
        for j, r in ready.items():
            if q in ops[j]["qs"] and max(r, free.get(q, 0.0)) <= st + 200.0 and (-bl[j], j) < (-bl[i], i):
                i = j
        st = max(ready.pop(i), free.get(q, 0.0))
        ops[i]["q"] = q
        free[q] = st + ops[i]["cost"]
        done[i] = free[q] + ops[i]["lat"]
        order.append(i)
        for s in succ[i]:
            left[s] -= 1
            if left[s] == 0:
                ready[s] = max(done[d] for d in ops[s]["deps"]) + HOP
    return order


def improve(ops, order, iters):
    n = len(ops)
    cost, lat = [o["cost"] for o in ops], [o["lat"] for o in ops]
    deps = [o["deps"] for o in ops]
    qof = [o["q"] for o in ops]

    def run(seq, qs):
        end, done, pred, free, lastq = [0.0] * n, [0.0] * n, [-1] * n, {}, {}
        for i in seq:
            q = qs[i]
            st, pr = free.get(q, 0.0), lastq.get(q, -1)
            for d in deps[i]:
                r = done[d] + HOP
                if r > st:
                    st, pr = r, d
            free[q] = end[i] = st + cost[i]
            done[i] = end[i] + lat[i]
            pred[i], lastq[q] = pr, i
        return done, pred
    done, pred = run(order, qof)
    best = cur = max(done)
    bo, bq = list(order), list(qof)
    order, seed = list(order), 12345
    for it in range(iters):
        seed = (seed * 1103515245 + 12345) % 2147483648
        path = []
        i = done.index(max(done))
        while i >= 0:
            path.append(i)
            i = pred[i]
        cand = [i for i in path if pred[i] >= 0 and pred[i] not in deps[i]] + [i for i in path if len(ops[i]["qs"]) > 1]
        if not cand:
            break
        i = cand[(seed >> 8) % len(cand)]
        nq, no = qof, list(order)
        if len(ops[i]["qs"]) > 1 and (seed >> 5) % 3 == 0:
            nq = list(qof)
            nq[i] = "S" if qof[i] == "V" else "V"
        else:
            j = pred[i]
            if j < 0 or j in deps[i]:
                continue
            a, b = no.index(j), no.index(i)
            need, head, tail = {i}, [], []
            for x in reversed(no[a:b + 1]):
                if x in need:
                    need.update(deps[x])
                    head.append(x)
                else:
                    tail.append(x)
            if j in need:
                continue
            no[a:b + 1] = head[::-1] + tail[::-1]
        d2, p2 = run(no, nq)
        m = max(d2)
        temp = TEMP * (1.0 - it / iters)
        if m <= cur or (seed >> 3) % 1000 < 1000.0 * 2.718281828 ** (-(m - cur) / (temp + 0.01)):
            order, qof, done, pred, cur = no, nq, d2, p2, m
            if m < best:
                best, bo, bq = m, list(no), list(nq)
    for o in ops:
        o["q"] = bq[o["i"]]
    return bo, best


PLAN = {}


def rank_program(g, core, T, topo):
    rank = T.rank_of(core)
    if rank is None:
        return
    ops = make_ops(g, T, topo, core, rank)
    depend(ops)
    if "order" not in PLAN:
        PLAN["order"], PLAN["best"] = improve(ops, schedule(ops), ITERS)
        PLAN["q"] = [o["q"] for o in ops]
    eng = {"V": g.vector, "S": g.scalar, "P": g.tensor, "G": g, "Y": g.sync}
    known = {q: {} for q in eng}
    count = {"V": 0, "S": 0, "P": 0, "G": 0}
    snap, token, stores, lsem = {}, {}, 0, 0
    for i in PLAN["order"]:
        o, q = ops[i], PLAN["q"][i]
        kn, toks = known[q], []
        for d in o["deps"]:
            if not (PLAN["q"][d] == "P" and q == "P"):
                toks += token[d]
        if o["skip"]:
            token[i] = toks
            continue
        for s, v in sorted(toks, key=lambda x: (-x[1], x[0])):
            if kn.get(s, 0) < v:
                eng[q].wait_ge(T.sem[s], v)
                kn[s] = v
                for s2, v2 in snap.get((s, v), {}).items():
                    kn[s2] = max(kn.get(s2, 0), v2)
        out = o["fn"](q)
        if out is None:
            lsem += 16
            token[i] = [(o["sem"], 16)]
            continue
        for x in out:
            x.then_inc(T.sem[o["sem"] or q], 16 if o["sem"] else 1)
        if o["sem"] == "st":
            stores += 16
            token[i] = []
            continue
        if o["sem"]:
            token[i] = [(o["sem"], 16 * len(out))]
        else:
            count[q] += len(out)
            token[i] = [(q, count[q])]
        snap[token[i][0]] = dict(kn)
    for s in sorted(count):
        g.wait_ge(T.sem[s], count[s])
    g.wait_ge(T.sem.lsem, lsem)
    g.wait_ge(T.sem.st, stores)
